import numpy as np
import ml_dtypes


def mxq(x, axis, fmt="e4m3"):
    dtype, down = {"e4m3": (ml_dtypes.float8_e4m3fn, 7), "e5m2": (ml_dtypes.float8_e5m2, 14)}[fmt]
    v = np.moveaxis(np.asarray(x, np.float32).astype(ml_dtypes.bfloat16).astype(np.float64), axis, -1)
    blocks = v.reshape(v.shape[:-1] + (-1, 32))
    amax = np.abs(blocks).max(-1, keepdims=True)
    byte = np.maximum(np.where(amax > 0, np.frexp(amax)[1] - 1 + 127, 0) - down, 1)
    scale = np.exp2(byte - 127.0)
    codes = (blocks / scale).astype(np.float32).astype(dtype).astype(np.float64)
    return np.moveaxis((codes * scale).reshape(v.shape), -1, axis)


WIDE = False


def mx_kscale(k):
    if not WIDE:
        return np.ones(k)
    levels = np.array([30, -30])
    if k % 512:
        return np.exp2(np.random.permutation(np.resize(levels, k // 32))).repeat(32)
    a = np.empty((k // 512, 16))
    for p in range(k // 512):
        a[p, :8] = np.random.permutation(np.resize(levels, 8))
        for g in range(8):
            far = levels[np.abs(levels - a[p, g]) >= 10]
            a[p, g + 8] = far[np.random.randint(len(far))]
    return np.exp2(a.ravel()).repeat(32)


def f64(x):
    return np.asarray(x).astype(np.float64)


def striped(idx):
    return np.tile(np.asarray(idx).reshape(-1, 16).T, (8, 1)).astype(np.uint16)


def unstriped(offs):
    return offs[:16].T.reshape(-1).astype(np.int64)


E2M1 = np.array([0.0, 0.5, 1.0, 1.5, 2.0, 3.0, 4.0, 6.0, -0.0, -0.5, -1.0, -1.5, -2.0, -3.0, -4.0, -6.0])


def pack_weight(w, fmt):
    k, n = w.shape
    w = f64(np.asarray(w, np.float32).astype(ml_dtypes.bfloat16)).reshape(k // 32, 32, n)
    amax = np.abs(w).max(1)
    if fmt in ("e4m3", "e5m2"):
        byte = np.frexp(amax)[1] - 1 + 127 - (7 if fmt == "e4m3" else 14)
    else:
        mant, ex = np.frexp(amax / 6.0)
        byte = np.where(mant > 0.5, ex, ex - 1) + 127
    byte = np.clip(np.where(amax > 0, byte, 1), 1, 254)
    scaled = (w * np.exp2(127.0 - byte)[:, None, :]).reshape(k, n).astype(np.float32)
    by_word = np.ascontiguousarray(scaled.reshape(k // 512, 128, 4, n).transpose(0, 1, 3, 2))
    if fmt in ("e4m3", "e5m2"):
        words = by_word.astype(ml_dtypes.float8_e4m3fn if fmt == "e4m3" else ml_dtypes.float8_e5m2).view(np.uint8)
    else:
        c = by_word.astype(ml_dtypes.float4_e2m1fn).view(np.uint8) & 0xF
        words = (c[..., 0::2] | (c[..., 1::2] << 4)).reshape(k // 512, 128, 2 * n)
    return np.ascontiguousarray(words), np.ascontiguousarray(byte.astype(np.uint8).reshape(k // 512, 16, n))


def unpack_weight(words, scales, fmt):
    g, _, n = scales.shape
    words = np.ascontiguousarray(words).reshape(g, 128, n, -1)
    if fmt in ("e4m3", "e5m2"):
        vals = words.view(ml_dtypes.float8_e4m3fn if fmt == "e4m3" else ml_dtypes.float8_e5m2).astype(np.float64)
    else:
        nib = np.empty((g, 128, n, 4), np.uint8)
        nib[..., 0::2] = words & 0xF
        nib[..., 1::2] = words >> 4
        vals = E2M1[nib]
    vals = vals * np.repeat(np.exp2(scales.astype(np.float64) - 127.0), 8, axis=1)[..., None]
    return vals.transpose(0, 1, 3, 2).reshape(g * 512, n)


def sigmoid(v):
    return 1.0 / (1.0 + np.exp(-v))


K, T, Z, J, R, C, O, N, E = 512, 1024, 1024, 256, 512, 512, 256, 256, 1024


def setup_inputs():
    n = np.random.standard_normal
    idx = np.random.permutation(T)[:J]
    idx2 = np.random.permutation(Z)[:J]
    idx3 = np.random.permutation(C)[:J]
    idx4 = np.random.permutation(C)[:J]
    idx5 = np.random.permutation(C)[:O]
    idx6 = np.random.permutation(C)[:O]
    idx7 = np.random.permutation(E)[:O]
    fk = mx_kscale(K)
    fr = mx_kscale(R)
    xtp = pack_weight(n((K, T)) / fk[:, None], "e5m2")
    xop = pack_weight(n((K, Z)) / fk[:, None], "e4m3")
    wp = pack_weight(n((K, R)) * 1 / np.sqrt(K) * fk[:, None] * fr, "e2m1")
    wbp = pack_weight(n((R, N)) * 1 / np.sqrt(R) / fr[:, None], "e2m1")
    return {
        "xt_words": xtp[0],
        "xt_scales": xtp[1],
        "xo_words": xop[0],
        "xo_scales": xop[1],
        "w_words": wp[0],
        "w_scales": wp[1],
        "wb_words": wbp[0],
        "wb_scales": wbp[1],
        "tz": (n((N, E))).astype(np.float32),
        "so": (np.random.uniform(0.6, 1.6, (N, 1))).astype(np.float32),
        "bo": (np.random.uniform(-1.0, 1.0, (N, 1))).astype(np.float32),
        "offs": striped(idx),
        "offs2": striped(idx2),
        "offs3": striped(idx3),
        "offs4": striped(idx4),
        "offs5": striped(idx5),
        "offs6": striped(idx6),
        "offs7": striped(idx7),
    }


def reference(xt_words, xt_scales, xo_words, xo_scales, w_words, w_scales, wb_words, wb_scales, tz, so, bo, offs, offs2, offs3, offs4, offs5, offs6, offs7):
    idx = unstriped(offs)
    idx2 = unstriped(offs2)
    idx3 = unstriped(offs3)
    idx4 = unstriped(offs4)
    idx5 = unstriped(offs5)
    idx6 = unstriped(offs6)
    idx7 = unstriped(offs7)
    xtu = unpack_weight(xt_words, xt_scales, "e5m2")
    xou = unpack_weight(xo_words, xo_scales, "e4m3")
    wu = unpack_weight(w_words, w_scales, "e2m1")
    wbu = unpack_weight(wb_words, wb_scales, "e2m1")
    xtidxg = xtu[:, idx]
    a = wu.T @ xtidxg
    xoidx2g = xou[:, idx2]
    b = wu.T @ xoidx2g
    pw = np.zeros((R, C))
    pw[:, idx3] = a
    pv = np.zeros((R, C))
    pv[:, idx4] = b
    hid = np.abs(pw[:, idx5] - pv[:, idx6])
    hidq = mxq(hid, 0, "e4m3")
    p = wbu.T @ hidq
    y = p * sigmoid(f64(tz)[:, idx7] * f64(so) + f64(bo))
    return y

@@ -1,0 +1,193 @@
+from contextlib import ExitStack
+
+import concourse.mybir as mybir
+
+K, T, Z, J, R, C, O, N, E = 512, 1024, 1024, 256, 512, 512, 256, 256, 1024
+FLOPS = 2 * (2 * K * R * J + R * N * O)
+
+F32 = mybir.dt.float32
+BF16 = mybir.dt.bfloat16
+I32 = mybir.dt.int32
+U32 = mybir.dt.uint32
+U16 = mybir.dt.uint16
+U8 = mybir.dt.uint8
+E4M3X4 = mybir.dt.float8_e4m3fn_x4
+E5M2X4 = mybir.dt.float8_e5m2_x4
+E2M1X4 = mybir.dt.float4_e2m1fn_x4
+ACT = mybir.ActivationFunctionType
+ALU = mybir.AluOpType
+P = 128
+PACK = 4
+HALF = O // 2
+
+
+def load_scale_rows(queue, plane, scales):
+    for q in range(4):
+        rows = scales[0, 4 * q : 4 * q + 4, :].bitcast(I32)
+        queue.dma_start(
+            out=plane[32 * q : 32 * (q + 1), :].bitcast(I32),
+            in_=rows.unsqueeze(0).to_broadcast([8, 4, rows.shape[1]]),
+        )
+
+
+def tile_list_oneforboth_twoboards_one_finalgate_kernel(
+    tc, xt_words, xt_scales, xo_words, xo_scales, w_words, w_scales, wb_words, wb_scales,
+    tz, so, bo, offs, offs2, offs3, offs4, offs5, offs6, offs7, out,
+):
+    nc = tc.nc
+    with ExitStack() as ctx:
+        lists = ctx.enter_context(tc.tile_pool(name="lists", bufs=1))
+        keep = ctx.enter_context(tc.tile_pool(name="keep", bufs=1))
+        psum = ctx.enter_context(tc.psum_pool(name="psum", bufs=1))
+
+        def load_list(src, name):
+            tile = lists.tile([P, J // 16], U16, name=name)
+            nc.sync.dma_start(tile[:], src)
+            return tile
+
+        xt_plane = keep.tile([P, T], U8, align_bytes=64)
+        w_plane = keep.tile([P, R], U8, align_bytes=64)
+        xo_plane = keep.tile([P, Z], U8, align_bytes=64)
+        wb_plane = keep.tile([P, N], U8, align_bytes=64)
+
+        token_list = load_list(offs, "token_list")
+        w_raw = keep.tile([P, 2 * R], U8, align_bytes=64)
+        nc.sync.dma_start(out=w_raw[:].bitcast(I32), in_=w_words[0].bitcast(I32))
+        load_scale_rows(nc.scalar, xt_plane, xt_scales)
+        xt_table = keep.tile([P, T], I32, align_bytes=64)
+        nc.sync.dma_start(out=xt_table[:], in_=xt_words[0].rearrange("p c r -> p (c r)").bitcast(I32))
+        load_scale_rows(nc.sync, w_plane, w_scales)
+        xo_table = keep.tile([P, Z], I32, align_bytes=64)
+        nc.sync.dma_start(out=xo_table[:], in_=xo_words[0].rearrange("p c r -> p (c r)").bitcast(I32))
+        put_w_list = load_list(offs3, "put_w_list")
+        note_list = load_list(offs2, "note_list")
+        load_scale_rows(nc.sync, xo_plane, xo_scales)
+        read_w_list = load_list(offs5, "read_w_list")
+        put_v_list = load_list(offs4, "put_v_list")
+        gate_list = load_list(offs7, "gate_list")
+        slope = keep.tile([P, 2], F32)
+        shift = keep.tile([P, 2], F32)
+        with nc.allow_non_contiguous_dma(reason="one value a partition"):
+            nc.gpsimd.dma_start(out=slope[:], in_=so.rearrange("(h p) one -> p (h one)", p=P))
+            nc.gpsimd.dma_start(out=shift[:], in_=bo.rearrange("(h p) one -> p (h one)", p=P))
+        tz_rows = []
+        for h in range(2):
+            rows = keep.tile([P, E], F32, name=f"tz_rows{h}")
+            nc.sync.dma_start(out=rows[:], in_=tz[P * h : P * (h + 1), :])
+            tz_rows.append(rows)
+        read_v_list = load_list(offs6, "read_v_list")
+        wb_codes = keep.tile([P, 2 * N], U8, align_bytes=64)
+        nc.sync.dma_start(out=wb_codes[:].bitcast(I32), in_=wb_words[0].bitcast(I32))
+        load_scale_rows(nc.sync, wb_plane, wb_scales)
+
+        board_w = [keep.tile([P, C], F32, name=f"board_w{t}") for t in range(PACK)]
+        for board in board_w:
+            nc.vector.memset(board[:], 0.0)
+        board_v = [keep.tile([P, C], F32, name=f"board_v{t}") for t in range(PACK)]
+        for board in board_v:
+            nc.vector.memset(board[:], 0.0)
+        warm_in = keep.tile([P, 1], F32)
+        warm_out = keep.tile([P, 1], F32)
+        nc.vector.memset(warm_in[:], 0.0)
+        nc.scalar.activation(out=warm_out[:], in_=warm_in[:], func=ACT.Sigmoid)
+
+        w_codes = keep.tile([P, 2 * R], U8, align_bytes=64)
+        w_dealt_plane = keep.tile([P, R], U8, align_bytes=64)
+        nc.vector.tensor_copy(
+            out=w_codes[:].bitcast(U16).rearrange("p (t c i) -> p c t i", t=PACK, i=8),
+            in_=w_raw[:].bitcast(U16).rearrange("p (c i t) -> p c t i", t=PACK, i=8),
+        )
+        nc.vector.tensor_copy(
+            out=w_dealt_plane[:].rearrange("p (t c i) -> p c t i", t=PACK, i=16),
+            in_=w_plane[:].rearrange("p (c i t) -> p c t i", t=PACK, i=16),
+        )
+
+        def first_product(table, plane, picks, fmt, name):
+            codes = keep.tile([P, J], U32, align_bytes=64, name=f"{name}_codes")
+            picked_plane = keep.tile([P, J], U8, align_bytes=64, name=f"{name}_picked_plane")
+            nc.vector.tensor_copy(out=codes[:], in_=table[:].bitcast(U32).indirect(picks[:]))
+            nc.vector.tensor_copy(out=picked_plane[:], in_=plane[:].indirect(picks[:]))
+            banks = []
+            for u in range(2):
+                bank = psum.tile([P, 2, J], F32, name=f"{name}_bank{u}")
+                for i in range(2):
+                    t = 2 * u + i
+                    nc.tensor.matmul_mx(
+                        out=bank[:, i, :],
+                        lhsT=w_codes[:, 2 * P * t : 2 * P * (t + 1)].bitcast(E2M1X4),
+                        lhsT_scale=w_dealt_plane[:, P * t : P * (t + 1)],
+                        rhs=codes[:].bitcast(fmt),
+                        rhs_scale=picked_plane[:],
+                        start=True,
+                        stop=True,
+                    )
+                banks.append(bank)
+            return banks
+
+        a_banks = first_product(xt_table, xt_plane, token_list, E5M2X4, "a")
+        a_sums = [keep.tile([P, 2, J], F32, name=f"a_sums{u}") for u in range(2)]
+        nc.scalar.copy(out=a_sums[0][:], in_=a_banks[0][:])
+        nc.scalar.copy(out=a_sums[1][:], in_=a_banks[1][:])
+        b_banks = first_product(xo_table, xo_plane, note_list, E4M3X4, "b")
+        b_sums = [keep.tile([P, 2, J], F32, name=f"b_sums{u}") for u in range(2)]
+        nc.vector.tensor_copy(out=b_sums[0][:], in_=b_banks[0][:])
+        nc.vector.tensor_copy(out=b_sums[1][:], in_=b_banks[1][:])
+
+        read_w = []
+        for t in range(PACK):
+            nc.scalar.activation(out=board_w[t][:].indirect(put_w_list[:]), in_=a_sums[t // 2][:, t % 2, :], func=ACT.Copy)
+            picked = keep.tile([P, O], F32, name=f"read_w{t}")
+            nc.scalar.activation(out=picked[:], in_=board_w[t][:].indirect(read_w_list[:]), func=ACT.Copy)
+            read_w.append(picked)
+
+        gates = keep.tile([P, 2, O], F32)
+        for h in range(2):
+            nc.scalar.activation(
+                out=gates[:, h, :], in_=tz_rows[h][:].indirect(gate_list[:]), func=ACT.Sigmoid,
+                bias=shift[:, h : h + 1], scale=slope[:, h : h + 1],
+            )
+
+        hid = [keep.tile([P, HALF, PACK], BF16, align_bytes=64, name=f"hid{g}") for g in range(2)]
+        diff = [keep.tile([P, 2, O], F32, name=f"diff{u}") for u in range(2)]
+        for t in range(PACK):
+            u, i = divmod(t, 2)
+            nc.vector.tensor_copy(out=board_v[t][:].indirect(put_v_list[:]), in_=b_sums[u][:, i, :])
+            pieces = 2 if t == PACK - 1 else 1
+            width = O // pieces
+            for g in range(pieces):
+                nc.vector.tensor_tensor(
+                    out=diff[u][:, i, g * width : (g + 1) * width],
+                    in0=board_v[t][:].indirect(read_v_list[:, g * width // 16 : (g + 1) * width // 16]),
+                    in1=read_w[t][:, g * width : (g + 1) * width],
+                    op=ALU.subtract,
+                )
+        for u in range(2):
+            for g in range(2):
+                nc.scalar.activation(
+                    out=hid[g][:, :, 2 * u : 2 * u + 2],
+                    in_=diff[u][:, :, g * HALF : (g + 1) * HALF].rearrange("p i o -> p o i"),
+                    func=ACT.Abs,
+                )
+
+        for g in range(2):
+            hid_codes = keep.tile([P, HALF], U32, align_bytes=64, name=f"hid_codes{g}")
+            hid_plane = keep.tile([P, HALF], U8, align_bytes=64, name=f"hid_plane{g}")
+            nc.vector.quantize_mx(
+                out=hid_codes[:].bitcast(E4M3X4), scales=hid_plane[:], in_=hid[g][:].rearrange("p o t -> p (o t)")
+            )
+            bank = psum.tile([P, 2, HALF], F32, name=f"p_bank{g}")
+            for h in range(2):
+                nc.tensor.matmul_mx(
+                    out=bank[:, h, :],
+                    lhsT=wb_codes[:, 2 * P * h : 2 * P * (h + 1)].bitcast(E2M1X4),
+                    lhsT_scale=wb_plane[:, P * h : P * (h + 1)],
+                    rhs=hid_codes[:].bitcast(E4M3X4),
+                    rhs_scale=hid_plane[:],
+                    start=True,
+                    stop=True,
+                )
+            result = keep.tile([P, 2, HALF], F32, name=f"result{g}")
+            nc.vector.tensor_tensor(out=result[:], in0=bank[:], in1=gates[:, :, g * HALF : (g + 1) * HALF], op=ALU.mult)
+            nc.sync.dma_start(
+                out=out[:, g * HALF : (g + 1) * HALF].rearrange("(h p) o -> p h o", p=P), in_=result[:]
+            )

@@ -19,10 +19,11 @@ ALU = mybir.AluOpType
 P = 128
 PACK = 4
 HALF = O // 2
+BANK_SLICES = ((0, 1), (1, 1), (2, 2))
 
 
-def load_scale_rows(queue, plane, scales):
-    for q in range(4):
+def load_scale_rows(queue, plane, scales, quadrants=range(4)):
+    for q in quadrants:
         rows = scales[0, 4 * q : 4 * q + 4, :].bitcast(I32)
         queue.dma_start(
             out=plane[32 * q : 32 * (q + 1), :].bitcast(I32),
@@ -47,16 +48,17 @@ def tile_list_oneforboth_twoboards_one_finalgate_kernel(
 
         xt_plane = keep.tile([P, T], U8, align_bytes=64)
         w_plane = keep.tile([P, R], U8, align_bytes=64)
-        xo_plane = keep.tile([P, Z], U8, align_bytes=64)
+        xo_plane = keep.tile([P, Z], U8, align_bytes=64, tag="xo_plane_then_a_sums")
         wb_plane = keep.tile([P, N], U8, align_bytes=64)
 
         token_list = load_list(offs, "token_list")
+        load_scale_rows(nc.sync, w_plane, w_scales, range(1))
         w_raw = keep.tile([P, 2 * R], U8, align_bytes=64)
         nc.sync.dma_start(out=w_raw[:].bitcast(I32), in_=w_words[0].bitcast(I32))
         load_scale_rows(nc.scalar, xt_plane, xt_scales)
         xt_table = keep.tile([P, T], I32, align_bytes=64)
         nc.sync.dma_start(out=xt_table[:], in_=xt_words[0].rearrange("p c r -> p (c r)").bitcast(I32))
-        load_scale_rows(nc.sync, w_plane, w_scales)
+        load_scale_rows(nc.sync, w_plane, w_scales, range(1, 4))
         xo_table = keep.tile([P, Z], I32, align_bytes=64)
         nc.sync.dma_start(out=xo_table[:], in_=xo_words[0].rearrange("p c r -> p (c r)").bitcast(I32))
         put_w_list = load_list(offs3, "put_w_list")
@@ -68,8 +70,8 @@ def tile_list_oneforboth_twoboards_one_finalgate_kernel(
         slope = keep.tile([P, 2], F32)
         shift = keep.tile([P, 2], F32)
         with nc.allow_non_contiguous_dma(reason="one value a partition"):
-            nc.gpsimd.dma_start(out=slope[:], in_=so.rearrange("(h p) one -> p (h one)", p=P))
-            nc.gpsimd.dma_start(out=shift[:], in_=bo.rearrange("(h p) one -> p (h one)", p=P))
+            nc.sync.dma_start(out=slope[:], in_=so.rearrange("(h p) one -> p (h one)", p=P))
+            nc.sync.dma_start(out=shift[:], in_=bo.rearrange("(h p) one -> p (h one)", p=P))
         tz_rows = []
         for h in range(2):
             rows = keep.tile([P, E], F32, name=f"tz_rows{h}")
@@ -80,27 +82,30 @@ def tile_list_oneforboth_twoboards_one_finalgate_kernel(
         nc.sync.dma_start(out=wb_codes[:].bitcast(I32), in_=wb_words[0].bitcast(I32))
         load_scale_rows(nc.sync, wb_plane, wb_scales)
 
-        board_w = [keep.tile([P, C], F32, name=f"board_w{t}") for t in range(PACK)]
+        board_w = [keep.tile([P, C + 1], F32, name=f"board_w{t}") for t in range(PACK)]
         for board in board_w:
             nc.vector.memset(board[:], 0.0)
         board_v = [keep.tile([P, C], F32, name=f"board_v{t}") for t in range(PACK)]
         for board in board_v:
-            nc.vector.memset(board[:], 0.0)
+            nc.gpsimd.memset(board[:], 0.0)
         warm_in = keep.tile([P, 1], F32)
         warm_out = keep.tile([P, 1], F32)
         nc.vector.memset(warm_in[:], 0.0)
         nc.scalar.activation(out=warm_out[:], in_=warm_in[:], func=ACT.Sigmoid)
 
         w_codes = keep.tile([P, 2 * R], U8, align_bytes=64)
-        w_dealt_plane = keep.tile([P, R], U8, align_bytes=64)
         nc.vector.tensor_copy(
             out=w_codes[:].bitcast(U16).rearrange("p (t c i) -> p c t i", t=PACK, i=8),
             in_=w_raw[:].bitcast(U16).rearrange("p (c i t) -> p c t i", t=PACK, i=8),
         )
-        nc.vector.tensor_copy(
-            out=w_dealt_plane[:].rearrange("p (t c i) -> p c t i", t=PACK, i=16),
-            in_=w_plane[:].rearrange("p (c i t) -> p c t i", t=PACK, i=16),
-        )
+        w_dealt_planes = []
+        for first, count in ((0, 1), (1, PACK - 1)):
+            dealt = keep.tile([P, count, P], U8, align_bytes=64, name=f"w_dealt_plane{first}")
+            nc.vector.tensor_copy(
+                out=dealt[:].rearrange("p t (c i) -> p c t i", i=16),
+                in_=w_plane[:].rearrange("p (c i t) -> p c t i", t=PACK, i=16)[:, :, first : first + count, :],
+            )
+            w_dealt_planes.extend(dealt[:, i, :] for i in range(count))
 
         def first_product(table, plane, picks, fmt, name):
             codes = keep.tile([P, J], U32, align_bytes=64, name=f"{name}_codes")
@@ -108,14 +113,14 @@ def tile_list_oneforboth_twoboards_one_finalgate_kernel(
             nc.vector.tensor_copy(out=codes[:], in_=table[:].bitcast(U32).indirect(picks[:]))
             nc.vector.tensor_copy(out=picked_plane[:], in_=plane[:].indirect(picks[:]))
             banks = []
-            for u in range(2):
-                bank = psum.tile([P, 2, J], F32, name=f"{name}_bank{u}")
-                for i in range(2):
-                    t = 2 * u + i
+            for first, count in BANK_SLICES:
+                bank = psum.tile([P, count, J], F32, name=f"{name}_bank{first}")
+                for i in range(count):
+                    t = first + i
                     nc.tensor.matmul_mx(
                         out=bank[:, i, :],
                         lhsT=w_codes[:, 2 * P * t : 2 * P * (t + 1)].bitcast(E2M1X4),
-                        lhsT_scale=w_dealt_plane[:, P * t : P * (t + 1)],
+                        lhsT_scale=w_dealt_planes[t],
                         rhs=codes[:].bitcast(fmt),
                         rhs_scale=picked_plane[:],
                         start=True,
@@ -124,18 +129,24 @@ def tile_list_oneforboth_twoboards_one_finalgate_kernel(
                 banks.append(bank)
             return banks
 
+        def copy_out(copy, bank, name, tag):
+            count = bank.shape[1]
+            staged = keep.tile([P, count, J], F32, align_bytes=64, name=name, tag=tag)
+            copy(out=staged[:], in_=bank[:])
+            return [staged[:, i, :] for i in range(count)]
+
         a_banks = first_product(xt_table, xt_plane, token_list, E5M2X4, "a")
-        a_sums = [keep.tile([P, 2, J], F32, name=f"a_sums{u}") for u in range(2)]
-        nc.scalar.copy(out=a_sums[0][:], in_=a_banks[0][:])
-        nc.scalar.copy(out=a_sums[1][:], in_=a_banks[1][:])
+        a_sums = copy_out(nc.scalar.copy, a_banks[0], "a_sums0", "a_sums0")
+        a_sums += copy_out(nc.scalar.copy, a_banks[1], "a_sums1", "a_sums1")
         b_banks = first_product(xo_table, xo_plane, note_list, E4M3X4, "b")
-        b_sums = [keep.tile([P, 2, J], F32, name=f"b_sums{u}") for u in range(2)]
-        nc.vector.tensor_copy(out=b_sums[0][:], in_=b_banks[0][:])
-        nc.vector.tensor_copy(out=b_sums[1][:], in_=b_banks[1][:])
+        a_sums += copy_out(nc.vector.tensor_copy, a_banks[2], "a_sums2", "xo_plane_then_a_sums")
+        b_sums = []
+        for first, bank in zip((0, 1, 2), b_banks):
+            b_sums += copy_out(nc.vector.tensor_copy, bank, f"b_sums{first}", f"b_sums{first}")
 
         read_w = []
         for t in range(PACK):
-            nc.scalar.activation(out=board_w[t][:].indirect(put_w_list[:]), in_=a_sums[t // 2][:, t % 2, :], func=ACT.Copy)
+            nc.scalar.activation(out=board_w[t][:].indirect(put_w_list[:]), in_=a_sums[t], func=ACT.Copy)
             picked = keep.tile([P, O], F32, name=f"read_w{t}")
             nc.scalar.activation(out=picked[:], in_=board_w[t][:].indirect(read_w_list[:]), func=ACT.Copy)
             read_w.append(picked)
@@ -151,7 +162,7 @@ def tile_list_oneforboth_twoboards_one_finalgate_kernel(
         diff = [keep.tile([P, 2, O], F32, name=f"diff{u}") for u in range(2)]
         for t in range(PACK):
             u, i = divmod(t, 2)
-            nc.vector.tensor_copy(out=board_v[t][:].indirect(put_v_list[:]), in_=b_sums[u][:, i, :])
+            nc.vector.tensor_copy(out=board_v[t][:].indirect(put_v_list[:]), in_=b_sums[t])
             pieces = 2 if t == PACK - 1 else 1
             width = O // pieces
             for g in range(pieces):

from contextlib import ExitStack

import concourse.mybir as mybir

K, T, Z, J, R, C, O, N, E = 512, 1024, 1024, 256, 512, 512, 256, 256, 1024
FLOPS = 2 * (2 * K * R * J + R * N * O)

F32 = mybir.dt.float32
BF16 = mybir.dt.bfloat16
I32 = mybir.dt.int32
U32 = mybir.dt.uint32
U16 = mybir.dt.uint16
U8 = mybir.dt.uint8
E4M3X4 = mybir.dt.float8_e4m3fn_x4
E5M2X4 = mybir.dt.float8_e5m2_x4
E2M1X4 = mybir.dt.float4_e2m1fn_x4
ACT = mybir.ActivationFunctionType
ALU = mybir.AluOpType
P = 128
PACK = 4
HALF = O // 2
BANK_SLICES = ((0, 1), (1, 1), (2, 2))


def load_scale_rows(queue, plane, scales, quadrants=range(4)):
    for q in quadrants:
        rows = scales[0, 4 * q : 4 * q + 4, :].bitcast(I32)
        queue.dma_start(
            out=plane[32 * q : 32 * (q + 1), :].bitcast(I32),
            in_=rows.unsqueeze(0).to_broadcast([8, 4, rows.shape[1]]),
        )


def tile_list_oneforboth_twoboards_one_finalgate_kernel(
    tc, xt_words, xt_scales, xo_words, xo_scales, w_words, w_scales, wb_words, wb_scales,
    tz, so, bo, offs, offs2, offs3, offs4, offs5, offs6, offs7, out,
):
    nc = tc.nc
    with ExitStack() as ctx:
        lists = ctx.enter_context(tc.tile_pool(name="lists", bufs=1))
        keep = ctx.enter_context(tc.tile_pool(name="keep", bufs=1))
        psum = ctx.enter_context(tc.psum_pool(name="psum", bufs=1))

        def load_list(src, name):
            tile = lists.tile([P, J // 16], U16, name=name)
            nc.sync.dma_start(tile[:], src)
            return tile

        xt_plane = keep.tile([P, T], U8, align_bytes=64)
        w_plane = keep.tile([P, R], U8, align_bytes=64)
        xo_plane = keep.tile([P, Z], U8, align_bytes=64, tag="xo_plane_then_a_sums")
        wb_plane = keep.tile([P, N], U8, align_bytes=64)

        token_list = load_list(offs, "token_list")
        load_scale_rows(nc.sync, w_plane, w_scales, range(1))
        w_raw = keep.tile([P, 2 * R], U8, align_bytes=64)
        nc.sync.dma_start(out=w_raw[:].bitcast(I32), in_=w_words[0].bitcast(I32))
        load_scale_rows(nc.scalar, xt_plane, xt_scales)
        xt_table = keep.tile([P, T], I32, align_bytes=64)
        nc.sync.dma_start(out=xt_table[:], in_=xt_words[0].rearrange("p c r -> p (c r)").bitcast(I32))
        load_scale_rows(nc.sync, w_plane, w_scales, range(1, 4))
        xo_table = keep.tile([P, Z], I32, align_bytes=64)
        nc.sync.dma_start(out=xo_table[:], in_=xo_words[0].rearrange("p c r -> p (c r)").bitcast(I32))
        put_w_list = load_list(offs3, "put_w_list")
        note_list = load_list(offs2, "note_list")
        load_scale_rows(nc.sync, xo_plane, xo_scales)
        read_w_list = load_list(offs5, "read_w_list")
        put_v_list = load_list(offs4, "put_v_list")
        gate_list = load_list(offs7, "gate_list")
        slope = keep.tile([P, 2], F32)
        shift = keep.tile([P, 2], F32)
        with nc.allow_non_contiguous_dma(reason="one value a partition"):
            nc.sync.dma_start(out=slope[:], in_=so.rearrange("(h p) one -> p (h one)", p=P))
            nc.sync.dma_start(out=shift[:], in_=bo.rearrange("(h p) one -> p (h one)", p=P))
        tz_rows = []
        for h in range(2):
            rows = keep.tile([P, E], F32, name=f"tz_rows{h}")
            nc.sync.dma_start(out=rows[:], in_=tz[P * h : P * (h + 1), :])
            tz_rows.append(rows)
        read_v_list = load_list(offs6, "read_v_list")
        wb_codes = keep.tile([P, 2 * N], U8, align_bytes=64)
        nc.sync.dma_start(out=wb_codes[:].bitcast(I32), in_=wb_words[0].bitcast(I32))
        load_scale_rows(nc.sync, wb_plane, wb_scales)

        board_w = [keep.tile([P, C + 1], F32, name=f"board_w{t}") for t in range(PACK)]
        for board in board_w:
            nc.vector.memset(board[:], 0.0)
        board_v = [keep.tile([P, C], F32, name=f"board_v{t}") for t in range(PACK)]
        for board in board_v:
            nc.gpsimd.memset(board[:], 0.0)
        warm_in = keep.tile([P, 1], F32)
        warm_out = keep.tile([P, 1], F32)
        nc.vector.memset(warm_in[:], 0.0)
        nc.scalar.activation(out=warm_out[:], in_=warm_in[:], func=ACT.Sigmoid)

        w_codes = keep.tile([P, 2 * R], U8, align_bytes=64)
        nc.vector.tensor_copy(
            out=w_codes[:].bitcast(U16).rearrange("p (t c i) -> p c t i", t=PACK, i=8),
            in_=w_raw[:].bitcast(U16).rearrange("p (c i t) -> p c t i", t=PACK, i=8),
        )
        w_dealt_planes = []
        for first, count in ((0, 1), (1, PACK - 1)):
            dealt = keep.tile([P, count, P], U8, align_bytes=64, name=f"w_dealt_plane{first}")
            nc.vector.tensor_copy(
                out=dealt[:].rearrange("p t (c i) -> p c t i", i=16),
                in_=w_plane[:].rearrange("p (c i t) -> p c t i", t=PACK, i=16)[:, :, first : first + count, :],
            )
            w_dealt_planes.extend(dealt[:, i, :] for i in range(count))

        def first_product(table, plane, picks, fmt, name):
            codes = keep.tile([P, J], U32, align_bytes=64, name=f"{name}_codes")
            picked_plane = keep.tile([P, J], U8, align_bytes=64, name=f"{name}_picked_plane")
            nc.vector.tensor_copy(out=codes[:], in_=table[:].bitcast(U32).indirect(picks[:]))
            nc.vector.tensor_copy(out=picked_plane[:], in_=plane[:].indirect(picks[:]))
            banks = []
            for first, count in BANK_SLICES:
                bank = psum.tile([P, count, J], F32, name=f"{name}_bank{first}")
                for i in range(count):
                    t = first + i
                    nc.tensor.matmul_mx(
                        out=bank[:, i, :],
                        lhsT=w_codes[:, 2 * P * t : 2 * P * (t + 1)].bitcast(E2M1X4),
                        lhsT_scale=w_dealt_planes[t],
                        rhs=codes[:].bitcast(fmt),
                        rhs_scale=picked_plane[:],
                        start=True,
                        stop=True,
                    )
                banks.append(bank)
            return banks

        def copy_out(copy, bank, name, tag):
            count = bank.shape[1]
            staged = keep.tile([P, count, J], F32, align_bytes=64, name=name, tag=tag)
            copy(out=staged[:], in_=bank[:])
            return [staged[:, i, :] for i in range(count)]

        a_banks = first_product(xt_table, xt_plane, token_list, E5M2X4, "a")
        a_sums = copy_out(nc.scalar.copy, a_banks[0], "a_sums0", "a_sums0")
        a_sums += copy_out(nc.scalar.copy, a_banks[1], "a_sums1", "a_sums1")
        b_banks = first_product(xo_table, xo_plane, note_list, E4M3X4, "b")
        a_sums += copy_out(nc.vector.tensor_copy, a_banks[2], "a_sums2", "xo_plane_then_a_sums")
        b_sums = []
        for first, bank in zip((0, 1, 2), b_banks):
            b_sums += copy_out(nc.vector.tensor_copy, bank, f"b_sums{first}", f"b_sums{first}")

        read_w = []
        for t in range(PACK):
            nc.scalar.activation(out=board_w[t][:].indirect(put_w_list[:]), in_=a_sums[t], func=ACT.Copy)
            picked = keep.tile([P, O], F32, name=f"read_w{t}")
            nc.scalar.activation(out=picked[:], in_=board_w[t][:].indirect(read_w_list[:]), func=ACT.Copy)
            read_w.append(picked)

        gates = keep.tile([P, 2, O], F32)
        for h in range(2):
            nc.scalar.activation(
                out=gates[:, h, :], in_=tz_rows[h][:].indirect(gate_list[:]), func=ACT.Sigmoid,
                bias=shift[:, h : h + 1], scale=slope[:, h : h + 1],
            )

        hid = [keep.tile([P, HALF, PACK], BF16, align_bytes=64, name=f"hid{g}") for g in range(2)]
        diff = [keep.tile([P, 2, O], F32, name=f"diff{u}") for u in range(2)]
        for t in range(PACK):
            u, i = divmod(t, 2)
            nc.vector.tensor_copy(out=board_v[t][:].indirect(put_v_list[:]), in_=b_sums[t])
            pieces = 2 if t == PACK - 1 else 1
            width = O // pieces
            for g in range(pieces):
                nc.vector.tensor_tensor(
                    out=diff[u][:, i, g * width : (g + 1) * width],
                    in0=board_v[t][:].indirect(read_v_list[:, g * width // 16 : (g + 1) * width // 16]),
                    in1=read_w[t][:, g * width : (g + 1) * width],
                    op=ALU.subtract,
                )
        for u in range(2):
            for g in range(2):
                nc.scalar.activation(
                    out=hid[g][:, :, 2 * u : 2 * u + 2],
                    in_=diff[u][:, :, g * HALF : (g + 1) * HALF].rearrange("p i o -> p o i"),
                    func=ACT.Abs,
                )

        for g in range(2):
            hid_codes = keep.tile([P, HALF], U32, align_bytes=64, name=f"hid_codes{g}")
            hid_plane = keep.tile([P, HALF], U8, align_bytes=64, name=f"hid_plane{g}")
            nc.vector.quantize_mx(
                out=hid_codes[:].bitcast(E4M3X4), scales=hid_plane[:], in_=hid[g][:].rearrange("p o t -> p (o t)")
            )
            bank = psum.tile([P, 2, HALF], F32, name=f"p_bank{g}")
            for h in range(2):
                nc.tensor.matmul_mx(
                    out=bank[:, h, :],
                    lhsT=wb_codes[:, 2 * P * h : 2 * P * (h + 1)].bitcast(E2M1X4),
                    lhsT_scale=wb_plane[:, P * h : P * (h + 1)],
                    rhs=hid_codes[:].bitcast(E4M3X4),
                    rhs_scale=hid_plane[:],
                    start=True,
                    stop=True,
                )
            result = keep.tile([P, 2, HALF], F32, name=f"result{g}")
            nc.vector.tensor_tensor(out=result[:], in0=bank[:], in1=gates[:, :, g * HALF : (g + 1) * HALF], op=ALU.mult)
            nc.sync.dma_start(
                out=out[:, g * HALF : (g + 1) * HALF].rearrange("(h p) o -> p h o", p=P), in_=result[:]
            )
